import numpy as np
import ml_dtypes


def mxq(x, axis, fmt="e4m3"):
    dtype, down = {"e4m3": (ml_dtypes.float8_e4m3fn, 7), "e5m2": (ml_dtypes.float8_e5m2, 14)}[fmt]
    v = np.moveaxis(np.asarray(x, np.float32).astype(ml_dtypes.bfloat16).astype(np.float64), axis, -1)
    blocks = v.reshape(v.shape[:-1] + (-1, 32))
    amax = np.abs(blocks).max(-1, keepdims=True)
    byte = np.maximum(np.where(amax > 0, np.frexp(amax)[1] - 1 + 127, 0) - down, 1)
    scale = np.exp2(byte - 127.0)
    codes = (blocks / scale).astype(np.float32).astype(dtype).astype(np.float64)
    return np.moveaxis((codes * scale).reshape(v.shape), -1, axis)


WIDE = False


def mx_kscale(k):
    if not WIDE:
        return np.ones(k)
    levels = np.array([10, -10, 5, -5, 0])
    if k % 512:
        return np.exp2(np.random.permutation(np.resize(levels, k // 32))).repeat(32)
    a = np.empty((k // 512, 16))
    for p in range(k // 512):
        a[p, :8] = np.random.permutation(np.resize(levels, 8))
        for g in range(8):
            far = levels[np.abs(levels - a[p, g]) >= 10]
            a[p, g + 8] = far[np.random.randint(len(far))]
    return np.exp2(a.ravel()).repeat(32)


BF16 = ml_dtypes.bfloat16


def bf(x):
    return np.asarray(x, np.float32).astype(BF16)


def f64(x):
    return np.asarray(x).astype(np.float64)


M, K, N, R, S = 1024, 512, 1536, 1024, 512

SLOPE = 0.2


def draw0():
    s, t, u = mx_kscale(K), mx_kscale(N), mx_kscale(M)
    return {"cond": bf(np.random.standard_normal((M, K)) * s),
            "w_gamma": bf(0.5 * np.random.standard_normal((K, N)) / np.sqrt(K) / s[:, None]),
            "b_gamma": bf(0.2 * np.random.standard_normal(N)),
            "w_beta": bf(0.5 * np.random.standard_normal((K, N)) / np.sqrt(K) / s[:, None] * t),
            "b_beta": bf(0.3 * np.random.standard_normal(N) * t),
            "feat": bf(np.random.standard_normal((M, N)) * t),
            "frame_gain": bf(np.random.uniform(0.5, 1.5, M) * u),
            "w_proj": bf(np.random.standard_normal((N, R)) / np.sqrt(N) / t[:, None]),
            "b_proj": bf(0.3 * np.random.standard_normal(R)),
            "frame_restore": bf(np.random.uniform(0.5, 1.5, M) / u),
            "w_pool": bf(np.random.standard_normal((S, M)) / np.sqrt(M) / u),
            "chan_gain": bf((1.0 + 0.1 * np.random.standard_normal(N)) / t)}


def core(cond, w_gamma, b_gamma, w_beta, b_beta, feat, frame_gain, w_proj, b_proj, frame_restore, w_pool, chan_gain):
    cq = mxq(f64(cond), 1, "e4m3")
    gamma = (cq @ mxq(f64(w_gamma), 0, "e4m3")) + f64(b_gamma)
    beta = (cq @ mxq(f64(w_beta), 0, "e4m3")) + f64(b_beta)
    f = f64(feat) * (1.0 + gamma) + beta
    h = np.maximum(f, SLOPE * f) * f64(frame_gain)[:, None]
    y = (mxq(h, 1, "e4m3") @ mxq(f64(w_proj), 0, "e4m3")) * f64(frame_restore)[:, None] + f64(b_proj)
    z = (mxq(f64(w_pool), 1, "e4m3") @ mxq(h, 0, "e4m3")) * f64(chan_gain)
    return y, z


def e4m3fn_bytes(y):
    return np.clip(np.asarray(y, np.float64), -448.0, 448.0).astype(np.float32).astype(ml_dtypes.float8_e4m3fn).view(np.uint8)


def e4m3fn_values(b):
    return np.asarray(b, np.uint8).view(ml_dtypes.float8_e4m3fn).astype(np.float64)


def setup_inputs():
    d = draw0()
    x0 = np.asarray(d['w_proj']).astype(np.float64)
    s = (np.max(np.abs(x0), axis=(1,), keepdims=True) / 448.0).astype(np.float32)
    out = {}
    for k, v in d.items():
        if k == 'w_proj':
            out['w_proj_bytes'] = e4m3fn_bytes(x0 / s.astype(np.float64))
            out['w_proj_scale'] = s
        else:
            out[k] = v
    return out


def reference(cond, w_gamma, b_gamma, w_beta, b_beta, feat, frame_gain, w_proj_bytes, w_proj_scale, b_proj, frame_restore, w_pool, chan_gain):
    return core(cond, w_gamma, b_gamma, w_beta, b_beta, feat, frame_gain, e4m3fn_values(w_proj_bytes) * w_proj_scale.astype(np.float64), b_proj, frame_restore, w_pool, chan_gain)

@@ -1,0 +1,540 @@
+from contextlib import ExitStack
+
+import concourse.mybir as mybir
+from concourse.masks import make_identity
+
+M, K, N, R, S = 1024, 512, 1536, 1024, 512
+SLOPE = 0.2
+
+FLOPS = 2 * (2 * M * K * N + M * N * R + S * M * N)
+
+F32 = mybir.dt.float32
+BF16 = mybir.dt.bfloat16
+U32 = mybir.dt.uint32
+U8 = mybir.dt.uint8
+FP8 = mybir.dt.float8_e4m3fn
+FP8X4 = mybir.dt.float8_e4m3fn_x4
+ALU = mybir.AluOpType
+ACT = mybir.ActivationFunctionType
+
+WPENG = "gggggg"
+P = 128
+PASS = 512
+FG = M // PASS
+CG = N // PASS
+
+
+def tile_film_modulated_projection_f6_kernel(
+    tc, cond, w_gamma, b_gamma, w_beta, b_beta, feat, frame_gain, w_proj_bytes,
+    w_proj_scale, b_proj, frame_restore, w_pool, chan_gain, y_out, z_out,
+):
+    nc = tc.nc
+    with ExitStack() as ctx:
+        const = ctx.enter_context(tc.tile_pool(name="const", bufs=1))
+        work = ctx.enter_context(tc.tile_pool(name="work", bufs=2))
+        psum = ctx.enter_context(tc.psum_pool(name="psum", bufs=2))
+
+        def codes(name, width=PASS):
+            c = const.tile([P, width], U32, name=name + "_codes", align_bytes=64)
+            s = const.tile([P, width], U8, name=name + "_scales", align_bytes=64)
+            return c, s
+
+        def quantize(dst, src, lo=0):
+            c, s = dst
+            nc.vector.quantize_mx(
+                out=c[:, lo : lo + PASS].bitcast(FP8X4), scales=s[:, lo : lo + PASS], in_=src
+            )
+
+        def group():
+            return work.tile([P, 4 * PASS], BF16, name="grp", tag="grp", bufs=4, align_bytes=64)
+
+        def bank(tag):
+            return psum.tile([P, PASS], F32, name="bank_" + tag, tag=tag, bufs=4)
+
+        def mx(out, lhs, lo, rhs, rlo, start, stop):
+            nc.tensor.matmul_mx(
+                out=out,
+                lhsT=lhs[0][:, lo : lo + P].bitcast(FP8X4),
+                lhsT_scale=lhs[1][:, lo : lo + P],
+                rhs=rhs[0][:, rlo : rlo + PASS].bitcast(FP8X4),
+                rhs_scale=rhs[1][:, rlo : rlo + PASS],
+                start=start,
+                stop=stop,
+            )
+
+        ctx.enter_context(tc.manual_schedule())
+
+        ident = const.tile([P, P], F32, name="ident")
+        make_identity(nc, ident[:])
+
+        cond_v = cond.rearrange("(g p t) k -> g p t k", p=P, t=4)
+        feat_v = feat.rearrange("(g p t) n -> g p t n", p=P, t=4)
+        wg_v = w_gamma.rearrange("(p j) n -> p j n", j=4)
+        wb_v = w_beta.rearrange("(p j) n -> p j n", j=4)
+        bytes_v = w_proj_bytes.rearrange("(g p j) r -> g p j r", p=P, j=4)
+        y_v = y_out.rearrange("(g p t) r -> g t p r", p=P, t=4)
+
+        cond_raw, feat_raw, wg_raw, wb_raw, wbytes, rows = {}, {}, {}, {}, {}, {}
+
+        def raw4(name):
+            return work.tile([P, 4, PASS], BF16, name=name, tag="raw4", bufs=4)
+
+        def raw8(name):
+            return work.tile([P, 4, 2 * PASS], BF16, name=name, tag="raw8", bufs=4)
+
+        def load_cond(g):
+            cond_raw[g] = raw4("cond_raw%d" % g)
+            nc.sync.dma_start(out=cond_raw[g][:], in_=cond_v[g])
+
+        def load_first(view, store, key, name):
+            t = raw4(name)
+            nc.sync.dma_start(out=t[:], in_=view[:, :, 0:PASS])
+            store[key] = (t, 0)
+
+        def load_rest(view, store, keys, name):
+            t = raw8(name)
+            nc.sync.dma_start(out=t[:], in_=view[:, :, PASS:N])
+            store[keys[0]], store[keys[1]] = (t, 0), (t, PASS)
+
+        def load_row(name, vec, width):
+            rows[name] = const.tile([P, width], BF16, name=name)
+            nc.sync.dma_start(out=rows[name][:], in_=vec.partition_broadcast(P))
+
+        load_cond(0)
+        load_first(wg_v, wg_raw, 0, "wg_raw0")
+        load_first(feat_v[0], feat_raw, (0, 0), "feat_raw00")
+        load_first(wb_v, wb_raw, 0, "wb_raw0")
+
+        bg_raw = const.tile([P, 2 * CG, 2], BF16, name="bg_raw")
+        bb_raw = const.tile([P, 2 * CG, 2], BF16, name="bb_raw")
+        gain_raw = const.tile([P, FG, 4], BF16, name="gain_raw")
+        rest_raw = const.tile([P, FG, 4], BF16, name="rest_raw")
+        wsc = const.tile([P, CG, 4], F32, name="wsc")
+        nc.scalar.dma_start(out=bg_raw[:], in_=b_gamma.rearrange("(a q e) -> q a e", q=P, e=2))
+        nc.scalar.dma_start(out=bb_raw[:], in_=b_beta.rearrange("(a q e) -> q a e", q=P, e=2))
+        nc.scalar.dma_start(out=gain_raw[:], in_=frame_gain.rearrange("(g p t) -> p g t", p=P, t=4))
+        nc.scalar.dma_start(out=rest_raw[:], in_=frame_restore.rearrange("(g p t) -> p g t", p=P, t=4))
+        nc.scalar.dma_start(
+            out=wsc[:], in_=w_proj_scale.rearrange("(g p j) o -> p g (j o)", p=P, j=4)
+        )
+
+        load_rest(wg_v, wg_raw, (1, 2), "wg_raw12")
+        load_rest(wb_v, wb_raw, (1, 2), "wb_raw12")
+        load_rest(feat_v[0], feat_raw, ((0, 1), (0, 2)), "feat_raw012")
+
+        bg1 = const.tile([P, 4 * CG], F32, name="bg1")
+        bb1 = const.tile([P, 4 * CG], F32, name="bb1")
+        sgn = const.tile([P, 4 * FG], F32, name="sgn")
+        absg = const.tile([P, 4 * FG], F32, name="absg")
+        rest = const.tile([P, 4 * FG], F32, name="rest")
+        gflat = gain_raw[:].rearrange("p g t -> p (g t)")
+        nc.gpsimd.tensor_scalar_add(bg1[:], bg_raw[:].rearrange("p a e -> p (a e)"), 1.0)
+        nc.gpsimd.tensor_scalar_add(bb1[:], bb_raw[:].rearrange("p a e -> p (a e)"), 0.0)
+        nc.gpsimd.tensor_scalar(sgn[:], gflat, 0.0, 2.0, op0=ALU.is_ge, op1=ALU.mult)
+        nc.gpsimd.tensor_scalar_add(sgn[:], sgn[:], -1.0)
+        nc.gpsimd.tensor_tensor(absg[:], sgn[:], gflat, op=ALU.mult)
+        nc.gpsimd.tensor_tensor(rest[:], sgn[:], rest_raw[:].rearrange("p g t -> p (g t)"), op=ALU.mult)
+
+        cond_q, wg_q, wb_q, wproj_q, pool_q, hf_q, hc_q = {}, {}, {}, {}, {}, {}, {}
+        groups = {}
+
+        def cond_turn(g):
+            words = cond_raw[g][:].bitcast(F32)
+            grp = groups["cond", g] = group()
+            gw = grp[:].bitcast(F32).rearrange("p (t f u) -> p t f u", t=4, u=2)
+            for h in range(2):
+                b = bank("turn")
+                for t2 in range(2):
+                    for u in range(2):
+                        lo = (2 * t2 + u) * P
+                        nc.tensor.transpose(b[:, lo : lo + P], words[:, 2 * h + t2, u::2], ident[:])
+                nc.scalar.copy(
+                    out=gw[:, 2 * h : 2 * h + 2],
+                    in_=b[:].rearrange("p (t u f) -> p t f u", t=2, u=2),
+                )
+
+        def cond_quant(g):
+            cond_q[g] = codes("cond%d" % g)
+            quantize(cond_q[g], groups["cond", g][:])
+
+        def mix(eng, dst, src):
+            if eng == "v":
+                nc.vector.tensor_copy(out=dst, in_=src)
+            elif eng == "s":
+                nc.scalar.copy(out=dst, in_=src)
+            else:
+                for lo in range(0, dst.shape[1], P):
+                    part = slice(lo, lo + P)
+                    nc.gpsimd.tensor_scalar(dst[:, part], src[:, part], 1.0, 0.0, op0=ALU.mult, op1=ALU.add)
+
+        def w_mix(which, raw, c, eng, e):
+            t, lo = raw[c]
+            if e == 0:
+                groups[which, c] = group()
+            grp = groups[which, c]
+            src = t[:, :, lo : lo + PASS].rearrange("p j (m e) -> p e m j", e=2)[:, e]
+            dst = grp[:].rearrange("p (e m j) -> p e m j", e=2, j=4)[:, e]
+            mix(eng, dst, src)
+
+        def w_quant(which, store, c):
+            store[c] = codes("%s%d" % (which, c))
+            quantize(store[c], groups[which, c][:])
+
+        def wp_widen(c, h):
+            wide = groups["wide", c, h] = work.tile([P, 4, PASS], BF16, name="wide", tag="wide", bufs=2)
+            for j in range(4):
+                nc.scalar.activation(
+                    out=wide[:, j, :],
+                    in_=wbytes[c][:, j, h * PASS : (h + 1) * PASS].bitcast(FP8),
+                    func=ACT.Copy,
+                    scale=wsc[:, c, j : j + 1],
+                )
+
+        def wp_mix(c, h, eng="v"):
+            grp = groups["wp", c, h] = group()
+            dst = grp[:].rearrange("p (r j) -> p r j", j=4)
+            src = groups["wide", c, h][:].rearrange("p j r -> p r j")
+            mix(eng, dst, src)
+
+        def wp_quant(c, h):
+            if h == 0:
+                wproj_q[c] = codes("wproj%d" % c, R)
+            quantize(wproj_q[c], groups["wp", c, h][:], h * PASS)
+
+        pool_raw = {}
+
+        def pool_sign(i):
+            t = pool_raw[0]
+            nc.vector.tensor_tensor(t[:, i, :], t[:, i, :], sgn_row[:], op=ALU.mult)
+
+        def pool_turn(g):
+            words = pool_raw[0][:].bitcast(F32)
+            grp = groups["pool", g] = group()
+            gw = grp[:].bitcast(F32).rearrange("p (i s u) -> p i s u", i=4, u=2)
+            for h in range(2):
+                b = bank("turn")
+                for i2 in range(2):
+                    for u in range(2):
+                        lo = (2 * i2 + u) * P
+                        nc.tensor.transpose(
+                            b[:, lo : lo + P],
+                            words[:, 2 * h + i2, 256 * g + u : 256 * (g + 1) : 2],
+                            ident[:],
+                        )
+                nc.scalar.copy(
+                    out=gw[:, 2 * h : 2 * h + 2],
+                    in_=b[:].rearrange("p (i u s) -> p i s u", i=2, u=2),
+                )
+
+        def pool_quant(g):
+            pool_q[g] = codes("pool%d" % g)
+            quantize(pool_q[g], groups["pool", g][:])
+
+        blocks = [(g, c) for g in range(FG) for c in range(CG)]
+        ft, pair, a_t, f_t, fm_t, hf_t, hc_t = {}, {}, {}, {}, {}, {}, {}
+
+        def feat_turn(b):
+            t, lo = feat_raw[blocks[b]]
+            words = t[:].bitcast(F32)
+            ft[b] = work.tile([P, 2, PASS], F32, name="feat_t", tag="feat_t", bufs=2)
+            for v in range(2):
+                ps = bank("turn")
+                for tt in range(4):
+                    w0 = lo // 2 + v * P
+                    nc.tensor.transpose(ps[:, tt * P : (tt + 1) * P], words[:, tt, w0 : w0 + P], ident[:])
+                nc.scalar.copy(out=ft[b][:, v, :], in_=ps[:])
+
+        def film_mx(b, i):
+            g, c = blocks[b]
+            e, v = i // 2, i % 2
+            pg, pb = bank("mx"), bank("mx")
+            mx(pg[:], wg_q[c], i * P, cond_q[g], 0, True, True)
+            mx(pb[:], wb_q[c], i * P, cond_q[g], 0, True, True)
+            pair[b, i] = (pg, pb)
+
+        def film_scale(b, i):
+            g, c = blocks[b]
+            e, v = i // 2, i % 2
+            idx = 4 * c + 2 * v + e
+            fb = ft[b][:, v, :].bitcast(BF16).rearrange("p (f e) -> p e f", e=2)
+            a_t[b, i] = work.tile([P, PASS], F32, name="a", tag="a", bufs=3)
+            nc.vector.scalar_tensor_tensor(
+                out=a_t[b, i][:], in0=pair[b, i][0][:], scalar=bg1[:, idx : idx + 1], in1=fb[:, e, :],
+                op0=ALU.add, op1=ALU.mult,
+            )
+
+        def film_shift(b, i):
+            g, c = blocks[b]
+            e, v = i // 2, i % 2
+            idx = 4 * c + 2 * v + e
+            f_t[b, i] = work.tile([P, PASS], F32, name="f", tag="f", bufs=8)
+            nc.vector.scalar_tensor_tensor(
+                out=f_t[b, i][:], in0=pair[b, i][1][:], scalar=bb1[:, idx : idx + 1], in1=a_t[b, i][:],
+                op0=ALU.add, op1=ALU.add,
+            )
+
+        def f_turn(b, t):
+            g, c = blocks[b]
+            if t == 0:
+                fm_t[b] = work.tile([P, 4, PASS], F32, name="fm", tag="fm", bufs=1)
+            ps = bank("turn")
+            for i in range(4):
+                nc.tensor.transpose(ps[:, i * P : (i + 1) * P], f_t[b, i][:, t * P : (t + 1) * P], ident[:])
+            nc.scalar.activation(
+                out=fm_t[b][:, t, :].rearrange("p (jh e q) -> p jh e q", jh=2, e=2),
+                in_=ps[:].rearrange("p (e q jh) -> p jh e q", e=2, jh=2),
+                func=ACT.Copy,
+                scale=absg[:, 4 * g + t : 4 * g + t + 1],
+            )
+
+        def leaky(b, lo=0, hi=PASS):
+            if lo == 0:
+                hf_t[b] = work.tile([P, 4 * PASS], BF16, name="hf", tag="hf", bufs=1, align_bytes=64)
+            src = fm_t[b][:, :, lo:hi].rearrange("p t c -> p c t")
+            nc.vector.scalar_tensor_tensor(
+                out=hf_t[b][:, 4 * lo : 4 * hi].rearrange("p (c t) -> p c t", t=4),
+                in0=src, scalar=SLOPE, in1=src, op0=ALU.mult, op1=ALU.max,
+            )
+
+        def hf_quant(b):
+            hf_q[blocks[b]] = codes("hf%d%d" % blocks[b])
+            quantize(hf_q[blocks[b]], hf_t[b][:])
+
+        def hc_turn(b, u):
+            if u == 0:
+                hc_t[b] = work.tile([P, 4 * PASS], BF16, name="hc", tag="hc", bufs=1, align_bytes=64)
+            words = hf_t[b][:].bitcast(F32)
+            ps = bank("turn")
+            for j in range(4):
+                nc.tensor.transpose(
+                    ps[:, j * P : (j + 1) * P], words[:, 256 * j + u : 256 * (j + 1) : 2], ident[:]
+                )
+            nc.scalar.copy(
+                out=hc_t[b][:, 1024 * u : 1024 * (u + 1)].rearrange("q (e p j) -> q e p j", e=2, j=4),
+                in_=ps[:].bitcast(BF16).rearrange("q (j p e) -> q e p j", j=4, e=2),
+            )
+
+        def hc_quant(b, u):
+            if u == 0:
+                hc_q[blocks[b]] = codes("hc%d%d" % blocks[b])
+            q = hc_q[blocks[b]]
+            nc.vector.quantize_mx(
+                out=q[0][:, 256 * u : 256 * (u + 1)].bitcast(FP8X4),
+                scales=q[1][:, 256 * u : 256 * (u + 1)],
+                in_=hc_t[b][:, 1024 * u : 1024 * (u + 1)],
+            )
+
+        ys_t, yb, zb = {}, {}, {}
+
+        def y_mx(g, t, h, c0=0, c1=CG, tag="mx"):
+            if c0 == 0:
+                yb[g, t, h] = bank(tag)
+            for c in range(c0, c1):
+                mx(yb[g, t, h][:], hc_q[g, c], t * P, wproj_q[c], h * PASS, c == 0, c == CG - 1)
+
+        def y_out_half(g, t, h):
+            if h == 0:
+                ys_t[g, t] = work.tile([P, R], F32, name="ys", tag="raw4", bufs=4)
+            ys = ys_t[g, t]
+            half = slice(h * PASS, (h + 1) * PASS)
+            scale = rest[:, 4 * g + t : 4 * g + t + 1]
+            if h == 0:
+                nc.vector.scalar_tensor_tensor(
+                    out=ys[:, half], in0=yb[g, t, h][:], scalar=scale,
+                    in1=rows["bias_row"][:, half], op0=ALU.mult, op1=ALU.add,
+                )
+            else:
+                nc.scalar.activation(out=ys[:, half], in_=yb[g, t, h][:], func=ACT.Copy, scale=scale)
+                nc.gpsimd.tensor_tensor(ys[:, half], ys[:, half], rows["bias_row"][:, half], op=ALU.add)
+            if h == 1:
+                nc.sync.dma_start(out=y_v[g, t], in_=ys[:])
+
+        def z_mx(c, i, tag="mx"):
+            zb[c, i] = bank(tag)
+            for g in range(FG):
+                mx(zb[c, i][:], pool_q[g], i * P, hf_q[g, c], 0, g == 0, g == FG - 1)
+
+        def z_store(c, i):
+            zs = work.tile([P, PASS], F32, name="zs", tag="zs", bufs=6)
+            nc.vector.tensor_tensor(
+                zs[:].rearrange("s (q j) -> s q j", j=4),
+                zb[c, i][:].rearrange("s (j q) -> s q j", j=4),
+                rows["cgain_row"][:, c * PASS : (c + 1) * PASS].rearrange("s (q j) -> s q j", j=4),
+                op=ALU.mult,
+            )
+            nc.sync.dma_start(out=z_out[i * P : (i + 1) * P, c * PASS : (c + 1) * PASS], in_=zs[:])
+
+        jobs, issued = [], []
+
+        def issue(n):
+            for _ in range(n):
+                if jobs:
+                    job = jobs.pop(0)
+                    job[0]()
+                    issued.append(job)
+
+        def drain(n=1):
+            for _ in range(n):
+                if issued:
+                    issued.pop(0)[1]()
+
+        def slot(fns=()):
+            for fn in fns:
+                fn()
+
+        def step(b, x):
+            slot(x.get(0, ()))
+            film_scale(b, 0)
+            film_scale(b, 1)
+            film_shift(b, 0)
+            film_mx(b, 2)
+            slot(x.get(1, ()))
+            film_shift(b, 1)
+            film_mx(b, 3)
+            film_scale(b, 2)
+            slot(x.get(2, ()))
+            if b + 1 < len(blocks):
+                feat_turn(b + 1)
+            if b > 0:
+                leaky(b - 1)
+                hc_turn(b - 1, 0)
+                hc_turn(b - 1, 1)
+            film_scale(b, 3)
+            film_shift(b, 2)
+            slot(x.get(3, ()))
+            if b + 1 < len(blocks):
+                film_mx(b + 1, 0)
+            if b > 0:
+                hf_quant(b - 1)
+            film_shift(b, 3)
+            slot(x.get(4, ()))
+            if b + 1 < len(blocks):
+                film_mx(b + 1, 1)
+            for t in range(4):
+                f_turn(b, t)
+            slot(x.get(5, ()))
+            if b > 0:
+                hc_quant(b - 1, 0)
+                hc_quant(b - 1, 1)
+            slot(x.get(6, ()))
+
+        def wmix(c, eng):
+            return [
+                lambda: w_mix("wg", wg_raw, c, eng, 0), lambda: w_mix("wg", wg_raw, c, eng, 1),
+                lambda: w_mix("wb", wb_raw, c, eng, 0), lambda: w_mix("wb", wb_raw, c, eng, 1),
+            ]
+
+        def wquant(c):
+            return [lambda: w_quant("wg", wg_q, c), lambda: w_quant("wb", wb_q, c)]
+
+        def load_w_proj(c):
+            wbytes[c] = const.tile([P, 4, R], U8, name="w_bytes%d" % c)
+            nc.sync.dma_start(out=wbytes[c][:], in_=bytes_v[c])
+
+        def load_pool():
+            pool_raw[0] = raw8("pool_raw")
+            nc.sync.dma_start(out=pool_raw[0][:], in_=w_pool.rearrange("(i s) m -> s i m", s=P))
+
+        sgn_row = const.tile([P, M], BF16, name="sgn_row")
+
+        def make_sign_row():
+            nc.gpsimd.tensor_scalar(sgn_row[:], rows["gain_row"][:], 0.0, 2.0, op0=ALU.is_ge, op1=ALU.mult)
+            nc.gpsimd.tensor_scalar(sgn_row[:], sgn_row[:], 1.0, -1.0, op0=ALU.mult, op1=ALU.add)
+
+        cond_turn(0)
+        w_mix("wg", wg_raw, 0, "v", 0)
+        w_mix("wg", wg_raw, 0, "s", 1)
+        cond_quant(0)
+        w_mix("wb", wb_raw, 0, "s", 0)
+        w_mix("wb", wb_raw, 0, "v", 1)
+        feat_turn(0)
+        w_quant("wg", wg_q, 0)
+        w_quant("wb", wb_q, 0)
+        film_mx(0, 0)
+        film_mx(0, 1)
+        for c in range(CG):
+            load_w_proj(c)
+        m1 = wmix(1, "s")[:2] + wmix(1, "g")[2:]
+        m2 = wmix(2, "s")[:2] + wmix(2, "g")[2:]
+        q1, q2 = wquant(1), wquant(2)
+
+        def wp(c, h, eng):
+            return [lambda: wp_widen(c, h)], [lambda: wp_mix(c, h, eng)], [lambda: wp_quant(c, h)]
+
+        wps = [wp(c, h, WPENG[2 * c + h]) for c in range(CG) for h in range(2)]
+        step(0, {0: m1, 3: q1, 5: m2})
+        load_cond(1)
+        load_first(feat_v[1], feat_raw, (1, 0), "feat_raw10")
+        load_pool()
+        load_row("gain_row", frame_gain, M)
+        make_sign_row()
+        step(1, {3: q2, 5: [lambda: cond_turn(1)] + wps[0][0] + wps[0][1] + wps[1][0]})
+        load_rest(feat_v[1], feat_raw, ((1, 1), (1, 2)), "feat_raw112")
+        load_row("bias_row", b_proj, R)
+        load_row("cgain_row", chan_gain, N)
+        step(2, {
+            0: wps[1][1], 3: [lambda: cond_quant(1)], 4: wps[0][2],
+            5: wps[2][0] + wps[2][1] + wps[3][0], 6: wps[1][2],
+        })
+        step(3, {
+            0: wps[3][1], 1: [lambda: pool_sign(0)], 2: [lambda: pool_sign(1)],
+            4: wps[2][2], 5: wps[4][0] + wps[4][1] + wps[5][0], 6: wps[3][2],
+        })
+        step(4, {
+            0: wps[5][1], 1: [lambda: pool_sign(2)], 2: [lambda: pool_sign(3)],
+            3: [lambda: pool_turn(0)], 4: wps[4][2] + [lambda: pool_turn(1)], 5: wps[5][2] + [lambda: pool_quant(0)],
+            6: [lambda: pool_quant(1)],
+        })
+
+        def add_y(g, lo, hi):
+            for t, h in [(t, h) for t in range(4) for h in range(2)][lo:hi]:
+                jobs.append((lambda t=t, h=h: y_mx(g, t, h), lambda t=t, h=h: y_out_half(g, t, h)))
+
+        def add_z(c):
+            for i in range(4):
+                jobs.append((lambda i=i: z_mx(c, i), lambda i=i: z_store(c, i)))
+
+        add_y(0, 0, 8)
+        add_z(0)
+        add_z(1)
+        go = [lambda: issue(1)]
+        out = [lambda: drain(1)]
+        step(5, {
+            0: go, 1: out + go, 2: out + go, 3: out + go, 4: go + out + go,
+            5: out + go + out + go + out + go, 6: out + go,
+        })
+        drain(1)
+        issue(1)
+        leaky(5)
+        hc_turn(5, 0)
+        hc_turn(5, 1)
+        drain(1)
+        issue(1)
+        hf_quant(5)
+        for k in range(12):
+            drain(1)
+            issue(1)
+        for k in range(4):
+            y_mx(1, k // 2, k % 2, 0, 2)
+        z_mx(2, 0, "turn")
+        z_mx(2, 1, "turn")
+        z_store(2, 0)
+        z_mx(2, 2, "turn")
+        hc_quant(5, 0)
+        for k in range(4):
+            y_mx(1, k // 2, k % 2, 2, 3)
+        z_store(2, 1)
+        z_mx(2, 3, "turn")
+        y_out_half(1, 0, 0)
+        y_out_half(1, 0, 1)
+        hc_quant(5, 1)
+        y_mx(1, 2, 0)
+        z_store(2, 2)
+        y_mx(1, 2, 1)
+        y_out_half(1, 1, 0)
+        y_out_half(1, 1, 1)
+        y_mx(1, 3, 0)
+        z_store(2, 3)
+        y_mx(1, 3, 1)
+        for k in range(4, 8):
+            y_out_half(1, k // 2, k % 2)

@@ -17,7 +17,10 @@ FP8X4 = mybir.dt.float8_e4m3fn_x4
 ALU = mybir.AluOpType
 ACT = mybir.ActivationFunctionType
 
-WPENG = "gggggg"
+ENG = {'wg00': 'v', 'wg01': 'v', 'wb00': 's', 'wb01': 'v', 'wm0': 'v', 'wm1': 'v', 'wm2': 'v', 'wm3': 'v', 'wm4': 'v', 'wm5': 's', 'wg10': 's', 'wb10': 's', 'wb21': 'v', 'wb11': 'v', 'wg11': 'v', 'wb20': 's', 'wg21': 'v', 'wg20': 's'}
+PLAN = [['wg10', 'wg11', 'wg20'], ['wb10', 'wb20 qwg1', 'wg21 wb11'], ['qwb1', '', ''], ['', 'wb21', 'wd0'], ['', '', ''], ['', '', ''], ['ct1 qwb2 wm0', 'cq1', 'qwg2'], ['wd2', '', 'wd1'], ['', 'ht00', 'hf0'], ['', '', ''], ['wm1 wd3', 'hq00 wd4', 'wm2 ht01'], ['', 'ht10', 'ht11 wq2'], ['wm3', '', 'hq10'], ['pt0 wq3', 'wd5', ''], ['hf1 hq11', '', ''], ['', 'wq0 wm5', 'wm4 ht20'], ['hq01', '', ''], ['', 'wq4', 'ht21 wq5'], ['wq1', '', 'pt1 hq20 hq21'], ['go go go hf2', 'out ht30 out', ''], ['', 'out go', ''], ['go', '', 'go out hf3'], ['', 'out', 'ht31 go'], ['pq0', 'hq30', 'out out'], ['pq1 ht40', 'go go', 'go go'], ['hq31 out go', 'ht41 hf4', 'out out'], ['', 'out go hq40', 'hf5 hq41 go out out']]
+TAIL = 'ht50 ht51 go out go out go out go out go out out go p0fin p1fin out p2mx p3mx hq50 f0 f1 f2 f3 p4turn p5turn o0 o1 hq51 f4 f5 o2 p6fin f6 o3 p7fin f7 o4 o5 o6 o7'
+YS = ''
 P = 128
 PASS = 512
 FG = M // PASS
@@ -46,10 +49,10 @@ def tile_film_modulated_projection_f6_kernel(
             )
 
         def group():
-            return work.tile([P, 4 * PASS], BF16, name="grp", tag="grp", bufs=4, align_bytes=64)
+            return work.tile([P, 4 * PASS], BF16, name="grp", tag="grp", bufs=5, align_bytes=64)
 
         def bank(tag):
-            return psum.tile([P, PASS], F32, name="bank_" + tag, tag=tag, bufs=4)
+            return psum.tile([P, PASS], F32, name="bank_" + tag, tag=tag, bufs=4 if tag == "mx" else 2)
 
         def mx(out, lhs, lo, rhs, rlo, start, stop):
             nc.tensor.matmul_mx(
@@ -124,16 +127,12 @@ def tile_film_modulated_projection_f6_kernel(
 
         bg1 = const.tile([P, 4 * CG], F32, name="bg1")
         bb1 = const.tile([P, 4 * CG], F32, name="bb1")
-        sgn = const.tile([P, 4 * FG], F32, name="sgn")
-        absg = const.tile([P, 4 * FG], F32, name="absg")
+        nc.gpsimd.tensor_scalar(bg1[:], bg_raw[:].rearrange("p a e -> p (a e)"), 1.0, 0.0, op0=ALU.add, op1=ALU.add)
+        nc.gpsimd.tensor_scalar(bb1[:], bb_raw[:].rearrange("p a e -> p (a e)"), 1.0, 0.0, op0=ALU.mult, op1=ALU.add)
+        gain = const.tile([P, 4 * FG], F32, name="gain")
         rest = const.tile([P, 4 * FG], F32, name="rest")
-        gflat = gain_raw[:].rearrange("p g t -> p (g t)")
-        nc.gpsimd.tensor_scalar_add(bg1[:], bg_raw[:].rearrange("p a e -> p (a e)"), 1.0)
-        nc.gpsimd.tensor_scalar_add(bb1[:], bb_raw[:].rearrange("p a e -> p (a e)"), 0.0)
-        nc.gpsimd.tensor_scalar(sgn[:], gflat, 0.0, 2.0, op0=ALU.is_ge, op1=ALU.mult)
-        nc.gpsimd.tensor_scalar_add(sgn[:], sgn[:], -1.0)
-        nc.gpsimd.tensor_tensor(absg[:], sgn[:], gflat, op=ALU.mult)
-        nc.gpsimd.tensor_tensor(rest[:], sgn[:], rest_raw[:].rearrange("p g t -> p (g t)"), op=ALU.mult)
+        nc.gpsimd.tensor_scalar(gain[:], gain_raw[:].rearrange("p g t -> p (g t)"), SLOPE, 0.0, op0=ALU.mult, op1=ALU.add)
+        nc.gpsimd.tensor_scalar(rest[:], rest_raw[:].rearrange("p g t -> p (g t)"), 1.0, 0.0, op0=ALU.mult, op1=ALU.add)
 
         cond_q, wg_q, wb_q, wproj_q, pool_q, hf_q, hc_q = {}, {}, {}, {}, {}, {}, {}
         groups = {}
@@ -181,7 +180,7 @@ def tile_film_modulated_projection_f6_kernel(
             quantize(store[c], groups[which, c][:])
 
         def wp_widen(c, h):
-            wide = groups["wide", c, h] = work.tile([P, 4, PASS], BF16, name="wide", tag="wide", bufs=2)
+            wide = groups["wide", c, h] = work.tile([P, 4, PASS], BF16, name="wide", tag="wide", bufs=3)
             for j in range(4):
                 nc.scalar.activation(
                     out=wide[:, j, :],
@@ -202,10 +201,6 @@ def tile_film_modulated_projection_f6_kernel(
             quantize(wproj_q[c], groups["wp", c, h][:], h * PASS)
 
         pool_raw = {}
-
-        def pool_sign(i):
-            t = pool_raw[0]
-            nc.vector.tensor_tensor(t[:, i, :], t[:, i, :], sgn_row[:], op=ALU.mult)
 
         def pool_turn(g):
             words = pool_raw[0][:].bitcast(F32)
@@ -231,7 +226,7 @@ def tile_film_modulated_projection_f6_kernel(
             quantize(pool_q[g], groups["pool", g][:])
 
         blocks = [(g, c) for g in range(FG) for c in range(CG)]
-        ft, pair, a_t, f_t, fm_t, hf_t, hc_t = {}, {}, {}, {}, {}, {}, {}
+        ft, pair, a_t, f_t, r_t, fb_t, hf_t, hc_t = {}, {}, {}, {}, {}, {}, {}, {}
 
         def feat_turn(b):
             t, lo = feat_raw[blocks[b]]
@@ -267,33 +262,39 @@ def tile_film_modulated_projection_f6_kernel(
             g, c = blocks[b]
             e, v = i // 2, i % 2
             idx = 4 * c + 2 * v + e
-            f_t[b, i] = work.tile([P, PASS], F32, name="f", tag="f", bufs=8)
+            f_t[b, i] = work.tile([P, PASS], F32, name="f", tag="f", bufs=5)
             nc.vector.scalar_tensor_tensor(
                 out=f_t[b, i][:], in0=pair[b, i][1][:], scalar=bb1[:, idx : idx + 1], in1=a_t[b, i][:],
                 op0=ALU.add, op1=ALU.add,
             )
 
-        def f_turn(b, t):
-            g, c = blocks[b]
-            if t == 0:
-                fm_t[b] = work.tile([P, 4, PASS], F32, name="fm", tag="fm", bufs=1)
-            ps = bank("turn")
-            for i in range(4):
-                nc.tensor.transpose(ps[:, i * P : (i + 1) * P], f_t[b, i][:, t * P : (t + 1) * P], ident[:])
-            nc.scalar.activation(
-                out=fm_t[b][:, t, :].rearrange("p (jh e q) -> p jh e q", jh=2, e=2),
-                in_=ps[:].rearrange("p (e q jh) -> p jh e q", e=2, jh=2),
-                func=ACT.Copy,
-                scale=absg[:, 4 * g + t : 4 * g + t + 1],
-            )
+        def relu(b, i):
+            r_t[b, i] = work.tile([P, PASS], F32, name="r", tag="r", bufs=4)
+            eng = ENG.get("relu%d%d" % (b, i), "s")
+            if eng == "g":
+                nc.gpsimd.tensor_scalar(r_t[b, i][:], f_t[b, i][:], 0.0, 1.0 / SLOPE - 1.0, op0=ALU.max, op1=ALU.mult)
+            elif eng == "s":
+                nc.scalar.activation(out=r_t[b, i][:], in_=f_t[b, i][:], func=ACT.Relu, scale=1.0 / SLOPE - 1.0)
+            else:
+                nc.vector.tensor_scalar(r_t[b, i][:], f_t[b, i][:], 0.0, 1.0 / SLOPE - 1.0, op0=ALU.max, op1=ALU.mult)
 
-        def leaky(b, lo=0, hi=PASS):
-            if lo == 0:
-                hf_t[b] = work.tile([P, 4 * PASS], BF16, name="hf", tag="hf", bufs=1, align_bytes=64)
-            src = fm_t[b][:, :, lo:hi].rearrange("p t c -> p c t")
-            nc.vector.scalar_tensor_tensor(
-                out=hf_t[b][:, 4 * lo : 4 * hi].rearrange("p (c t) -> p c t", t=4),
-                in0=src, scalar=SLOPE, in1=src, op0=ALU.mult, op1=ALU.max,
+        def f_turn(b, i):
+            ps = fb_t[b, i] = bank("fin")
+            for t in range(4):
+                part = slice(t * P, (t + 1) * P)
+                nc.tensor.matmul(ps[:, part], f_t[b, i][:, part], ident[:], start=True, stop=False, is_transpose=True)
+                nc.tensor.matmul(ps[:, part], r_t[b, i][:, part], ident[:], start=False, stop=True, is_transpose=True)
+
+        def finish(b, i):
+            g, c = blocks[b]
+            e, v = i // 2, i % 2
+            if i == 0:
+                hf_t[b] = work.tile([P, 4 * PASS], BF16, name="hf", tag="hf", bufs=2, align_bytes=64)
+            nc.vector.tensor_tensor(
+                hf_t[b][:].rearrange("p (jh e v qh t) -> p jh e v qh t", jh=2, e=2, v=2, t=4)[:, :, e, v],
+                fb_t[b, i][:].rearrange("p (t qh jh) -> p jh qh t", t=4, jh=2),
+                gain[:, 4 * g : 4 * g + 4].unsqueeze(1).unsqueeze(1).to_broadcast([P, 2, 64, 4]),
+                op=ALU.mult,
             )
 
         def hf_quant(b):
@@ -302,7 +303,7 @@ def tile_film_modulated_projection_f6_kernel(
 
         def hc_turn(b, u):
             if u == 0:
-                hc_t[b] = work.tile([P, 4 * PASS], BF16, name="hc", tag="hc", bufs=1, align_bytes=64)
+                hc_t[b] = work.tile([P, 4 * PASS], BF16, name="hc", tag="hc", bufs=2, align_bytes=64)
             words = hf_t[b][:].bitcast(F32)
             ps = bank("turn")
             for j in range(4):
@@ -338,7 +339,7 @@ def tile_film_modulated_projection_f6_kernel(
             ys = ys_t[g, t]
             half = slice(h * PASS, (h + 1) * PASS)
             scale = rest[:, 4 * g + t : 4 * g + t + 1]
-            if h == 0:
+            if ENG.get("y%d%d%d" % (g, t, h), "v") == "v":
                 nc.vector.scalar_tensor_tensor(
                     out=ys[:, half], in0=yb[g, t, h][:], scalar=scale,
                     in1=rows["bias_row"][:, half], op0=ALU.mult, op1=ALU.add,
@@ -356,12 +357,14 @@ def tile_film_modulated_projection_f6_kernel(
 
         def z_store(c, i):
             zs = work.tile([P, PASS], F32, name="zs", tag="zs", bufs=6)
-            nc.vector.tensor_tensor(
-                zs[:].rearrange("s (q j) -> s q j", j=4),
-                zb[c, i][:].rearrange("s (j q) -> s q j", j=4),
-                rows["cgain_row"][:, c * PASS : (c + 1) * PASS].rearrange("s (q j) -> s q j", j=4),
-                op=ALU.mult,
-            )
+            row = rows["cgain_row"][:, c * PASS : (c + 1) * PASS]
+            zn = zs[:].rearrange("s (q j) -> s q j", j=4)
+            zp = zb[c, i][:].rearrange("s (j q) -> s q j", j=4)
+            if ENG.get("z%d%d" % (c, i), "v") == "v":
+                nc.vector.tensor_tensor(zn, zp, row.rearrange("s (q j) -> s q j", j=4), op=ALU.mult)
+            else:
+                nc.scalar.copy(out=zn, in_=zp)
+                nc.gpsimd.tensor_tensor(zs[:], zs[:], row, op=ALU.mult)
             nc.sync.dma_start(out=z_out[i * P : (i + 1) * P, c * PASS : (c + 1) * PASS], in_=zs[:])
 
         jobs, issued = [], []
@@ -382,51 +385,6 @@ def tile_film_modulated_projection_f6_kernel(
             for fn in fns:
                 fn()
 
-        def step(b, x):
-            slot(x.get(0, ()))
-            film_scale(b, 0)
-            film_scale(b, 1)
-            film_shift(b, 0)
-            film_mx(b, 2)
-            slot(x.get(1, ()))
-            film_shift(b, 1)
-            film_mx(b, 3)
-            film_scale(b, 2)
-            slot(x.get(2, ()))
-            if b + 1 < len(blocks):
-                feat_turn(b + 1)
-            if b > 0:
-                leaky(b - 1)
-                hc_turn(b - 1, 0)
-                hc_turn(b - 1, 1)
-            film_scale(b, 3)
-            film_shift(b, 2)
-            slot(x.get(3, ()))
-            if b + 1 < len(blocks):
-                film_mx(b + 1, 0)
-            if b > 0:
-                hf_quant(b - 1)
-            film_shift(b, 3)
-            slot(x.get(4, ()))
-            if b + 1 < len(blocks):
-                film_mx(b + 1, 1)
-            for t in range(4):
-                f_turn(b, t)
-            slot(x.get(5, ()))
-            if b > 0:
-                hc_quant(b - 1, 0)
-                hc_quant(b - 1, 1)
-            slot(x.get(6, ()))
-
-        def wmix(c, eng):
-            return [
-                lambda: w_mix("wg", wg_raw, c, eng, 0), lambda: w_mix("wg", wg_raw, c, eng, 1),
-                lambda: w_mix("wb", wb_raw, c, eng, 0), lambda: w_mix("wb", wb_raw, c, eng, 1),
-            ]
-
-        def wquant(c):
-            return [lambda: w_quant("wg", wg_q, c), lambda: w_quant("wb", wb_q, c)]
-
         def load_w_proj(c):
             wbytes[c] = const.tile([P, 4, R], U8, name="w_bytes%d" % c)
             nc.sync.dma_start(out=wbytes[c][:], in_=bytes_v[c])
@@ -435,56 +393,27 @@ def tile_film_modulated_projection_f6_kernel(
             pool_raw[0] = raw8("pool_raw")
             nc.sync.dma_start(out=pool_raw[0][:], in_=w_pool.rearrange("(i s) m -> s i m", s=P))
 
-        sgn_row = const.tile([P, M], BF16, name="sgn_row")
-
-        def make_sign_row():
-            nc.gpsimd.tensor_scalar(sgn_row[:], rows["gain_row"][:], 0.0, 2.0, op0=ALU.is_ge, op1=ALU.mult)
-            nc.gpsimd.tensor_scalar(sgn_row[:], sgn_row[:], 1.0, -1.0, op0=ALU.mult, op1=ALU.add)
-
-        cond_turn(0)
-        w_mix("wg", wg_raw, 0, "v", 0)
-        w_mix("wg", wg_raw, 0, "s", 1)
-        cond_quant(0)
-        w_mix("wb", wb_raw, 0, "s", 0)
-        w_mix("wb", wb_raw, 0, "v", 1)
-        feat_turn(0)
-        w_quant("wg", wg_q, 0)
-        w_quant("wb", wb_q, 0)
-        film_mx(0, 0)
-        film_mx(0, 1)
+        extras = {"go": lambda: issue(1), "out": lambda: drain(1)}
         for c in range(CG):
-            load_w_proj(c)
-        m1 = wmix(1, "s")[:2] + wmix(1, "g")[2:]
-        m2 = wmix(2, "s")[:2] + wmix(2, "g")[2:]
-        q1, q2 = wquant(1), wquant(2)
+            for which, raw, store in (("wg", wg_raw, wg_q), ("wb", wb_raw, wb_q)):
+                for e in range(2):
+                    n = "%s%d%d" % (which, c, e)
+                    extras[n] = lambda which=which, raw=raw, c=c, e=e, n=n: w_mix(which, raw, c, ENG.get(n, "s"), e)
+                extras["q%s%d" % (which, c)] = lambda which=which, store=store, c=c: w_quant(which, store, c)
+            for h in range(2):
+                k = 2 * c + h
+                extras["wd%d" % k] = lambda c=c, h=h: wp_widen(c, h)
+                extras["wm%d" % k] = lambda c=c, h=h, k=k: wp_mix(c, h, ENG.get("wm%d" % k, "v"))
+                extras["wq%d" % k] = lambda c=c, h=h: wp_quant(c, h)
+        for g in range(FG):
+            extras["ct%d" % g] = lambda g=g: cond_turn(g)
+            extras["cq%d" % g] = lambda g=g: cond_quant(g)
+            extras["pt%d" % g] = lambda g=g: pool_turn(g)
+            extras["pq%d" % g] = lambda g=g: pool_quant(g)
 
-        def wp(c, h, eng):
-            return [lambda: wp_widen(c, h)], [lambda: wp_mix(c, h, eng)], [lambda: wp_quant(c, h)]
-
-        wps = [wp(c, h, WPENG[2 * c + h]) for c in range(CG) for h in range(2)]
-        step(0, {0: m1, 3: q1, 5: m2})
-        load_cond(1)
-        load_first(feat_v[1], feat_raw, (1, 0), "feat_raw10")
-        load_pool()
-        load_row("gain_row", frame_gain, M)
-        make_sign_row()
-        step(1, {3: q2, 5: [lambda: cond_turn(1)] + wps[0][0] + wps[0][1] + wps[1][0]})
-        load_rest(feat_v[1], feat_raw, ((1, 1), (1, 2)), "feat_raw112")
-        load_row("bias_row", b_proj, R)
-        load_row("cgain_row", chan_gain, N)
-        step(2, {
-            0: wps[1][1], 3: [lambda: cond_quant(1)], 4: wps[0][2],
-            5: wps[2][0] + wps[2][1] + wps[3][0], 6: wps[1][2],
-        })
-        step(3, {
-            0: wps[3][1], 1: [lambda: pool_sign(0)], 2: [lambda: pool_sign(1)],
-            4: wps[2][2], 5: wps[4][0] + wps[4][1] + wps[5][0], 6: wps[3][2],
-        })
-        step(4, {
-            0: wps[5][1], 1: [lambda: pool_sign(2)], 2: [lambda: pool_sign(3)],
-            3: [lambda: pool_turn(0)], 4: wps[4][2] + [lambda: pool_turn(1)], 5: wps[5][2] + [lambda: pool_quant(0)],
-            6: [lambda: pool_quant(1)],
-        })
+        def do(names):
+            for n in names.split():
+                extras[n]()
 
         def add_y(g, lo, hi):
             for t, h in [(t, h) for t in range(4) for h in range(2)][lo:hi]:
@@ -497,44 +426,61 @@ def tile_film_modulated_projection_f6_kernel(
         add_y(0, 0, 8)
         add_z(0)
         add_z(1)
-        go = [lambda: issue(1)]
-        out = [lambda: drain(1)]
-        step(5, {
-            0: go, 1: out + go, 2: out + go, 3: out + go, 4: go + out + go,
-            5: out + go + out + go + out + go, 6: out + go,
-        })
-        drain(1)
-        issue(1)
-        leaky(5)
-        hc_turn(5, 0)
-        hc_turn(5, 1)
-        drain(1)
-        issue(1)
-        hf_quant(5)
-        for k in range(12):
-            drain(1)
-            issue(1)
-        for k in range(4):
-            y_mx(1, k // 2, k % 2, 0, 2)
-        z_mx(2, 0, "turn")
-        z_mx(2, 1, "turn")
-        z_store(2, 0)
-        z_mx(2, 2, "turn")
-        hc_quant(5, 0)
-        for k in range(4):
-            y_mx(1, k // 2, k % 2, 2, 3)
-        z_store(2, 1)
-        z_mx(2, 3, "turn")
-        y_out_half(1, 0, 0)
-        y_out_half(1, 0, 1)
-        hc_quant(5, 1)
-        y_mx(1, 2, 0)
-        z_store(2, 2)
-        y_mx(1, 2, 1)
-        y_out_half(1, 1, 0)
-        y_out_half(1, 1, 1)
-        y_mx(1, 3, 0)
-        z_store(2, 3)
-        y_mx(1, 3, 1)
-        for k in range(4, 8):
-            y_out_half(1, k // 2, k % 2)
+        add_z(2)
+
+        tiles = [(b, i) for b in range(len(blocks)) for i in range(4)]
+        NT = len(tiles)
+
+        def loads(n):
+            if n == 2:
+                load_cond(1)
+                load_first(feat_v[1], feat_raw, (1, 0), "feat_raw10")
+                load_pool()
+            if n == 6:
+                load_rest(feat_v[1], feat_raw, ((1, 1), (1, 2)), "feat_raw112")
+                load_row("bias_row", b_proj, R)
+                load_row("cgain_row", chan_gain, N)
+
+        def stage(n, x):
+            if n < NT:
+                film_scale(*tiles[n])
+            do(x[0])
+            if 0 <= n - 1 < NT:
+                film_shift(*tiles[n - 1])
+            if 0 <= n + 1 < NT:
+                film_mx(*tiles[n + 1])
+            if 0 <= n - 1 < NT:
+                relu(*tiles[n - 1])
+            if n % 4 == 1 and n // 4 + 1 < len(blocks):
+                feat_turn(n // 4 + 1)
+            if 0 <= n - 2 < NT:
+                f_turn(*tiles[n - 2])
+            do(x[1])
+            if 0 <= n - 3 < NT:
+                finish(*tiles[n - 3])
+            do(x[2])
+            loads(n)
+
+        for k in range(8):
+            for tag in ("mx", "turn", "fin"):
+                extras["p%d%s" % (k, tag)] = lambda k=k, tag=tag: y_mx(1, k // 2, k % 2, 0, 2, tag)
+            extras["f%d" % k] = lambda k=k: y_mx(1, k // 2, k % 2, 2, 3)
+            extras["o%d" % k] = lambda k=k: y_out_half(1, k // 2, k % 2)
+        for b in range(len(blocks)):
+            extras["hf%d" % b] = lambda b=b: hf_quant(b)
+            for u in range(2):
+                extras["ht%d%d" % (b, u)] = lambda b=b, u=u: hc_turn(b, u)
+                extras["hq%d%d" % (b, u)] = lambda b=b, u=u: hc_quant(b, u)
+
+        cond_turn(0)
+        do("wg00 wg01")
+        cond_quant(0)
+        do("wb00 wb01")
+        feat_turn(0)
+        do("qwg0 qwb0")
+        film_mx(*tiles[0])
+        for c in range(CG):
+            load_w_proj(c)
+        for n in range(NT + 3):
+            stage(n, PLAN[n])
+        do(TAIL)

from contextlib import ExitStack

import concourse.mybir as mybir
from concourse.masks import make_identity

M, K, N, R, S = 1024, 512, 1536, 1024, 512
SLOPE = 0.2

FLOPS = 2 * (2 * M * K * N + M * N * R + S * M * N)

F32 = mybir.dt.float32
BF16 = mybir.dt.bfloat16
U32 = mybir.dt.uint32
U8 = mybir.dt.uint8
FP8 = mybir.dt.float8_e4m3fn
FP8X4 = mybir.dt.float8_e4m3fn_x4
ALU = mybir.AluOpType
ACT = mybir.ActivationFunctionType

ENG = {'wg00': 'v', 'wg01': 'v', 'wb00': 's', 'wb01': 'v', 'wm0': 'v', 'wm1': 'v', 'wm2': 'v', 'wm3': 'v', 'wm4': 'v', 'wm5': 's', 'wg10': 's', 'wb10': 's', 'wb21': 'v', 'wb11': 'v', 'wg11': 'v', 'wb20': 's', 'wg21': 'v', 'wg20': 's'}
PLAN = [['wg10', 'wg11', 'wg20'], ['wb10', 'wb20 qwg1', 'wg21 wb11'], ['qwb1', '', ''], ['', 'wb21', 'wd0'], ['', '', ''], ['', '', ''], ['ct1 qwb2 wm0', 'cq1', 'qwg2'], ['wd2', '', 'wd1'], ['', 'ht00', 'hf0'], ['', '', ''], ['wm1 wd3', 'hq00 wd4', 'wm2 ht01'], ['', 'ht10', 'ht11 wq2'], ['wm3', '', 'hq10'], ['pt0 wq3', 'wd5', ''], ['hf1 hq11', '', ''], ['', 'wq0 wm5', 'wm4 ht20'], ['hq01', '', ''], ['', 'wq4', 'ht21 wq5'], ['wq1', '', 'pt1 hq20 hq21'], ['go go go hf2', 'out ht30 out', ''], ['', 'out go', ''], ['go', '', 'go out hf3'], ['', 'out', 'ht31 go'], ['pq0', 'hq30', 'out out'], ['pq1 ht40', 'go go', 'go go'], ['hq31 out go', 'ht41 hf4', 'out out'], ['', 'out go hq40', 'hf5 hq41 go out out']]
TAIL = 'ht50 ht51 go out go out go out go out go out out go p0fin p1fin out p2mx p3mx hq50 f0 f1 f2 f3 p4turn p5turn o0 o1 hq51 f4 f5 o2 p6fin f6 o3 p7fin f7 o4 o5 o6 o7'
YS = ''
P = 128
PASS = 512
FG = M // PASS
CG = N // PASS


def tile_film_modulated_projection_f6_kernel(
    tc, cond, w_gamma, b_gamma, w_beta, b_beta, feat, frame_gain, w_proj_bytes,
    w_proj_scale, b_proj, frame_restore, w_pool, chan_gain, y_out, z_out,
):
    nc = tc.nc
    with ExitStack() as ctx:
        const = ctx.enter_context(tc.tile_pool(name="const", bufs=1))
        work = ctx.enter_context(tc.tile_pool(name="work", bufs=2))
        psum = ctx.enter_context(tc.psum_pool(name="psum", bufs=2))

        def codes(name, width=PASS):
            c = const.tile([P, width], U32, name=name + "_codes", align_bytes=64)
            s = const.tile([P, width], U8, name=name + "_scales", align_bytes=64)
            return c, s

        def quantize(dst, src, lo=0):
            c, s = dst
            nc.vector.quantize_mx(
                out=c[:, lo : lo + PASS].bitcast(FP8X4), scales=s[:, lo : lo + PASS], in_=src
            )

        def group():
            return work.tile([P, 4 * PASS], BF16, name="grp", tag="grp", bufs=5, align_bytes=64)

        def bank(tag):
            return psum.tile([P, PASS], F32, name="bank_" + tag, tag=tag, bufs=4 if tag == "mx" else 2)

        def mx(out, lhs, lo, rhs, rlo, start, stop):
            nc.tensor.matmul_mx(
                out=out,
                lhsT=lhs[0][:, lo : lo + P].bitcast(FP8X4),
                lhsT_scale=lhs[1][:, lo : lo + P],
                rhs=rhs[0][:, rlo : rlo + PASS].bitcast(FP8X4),
                rhs_scale=rhs[1][:, rlo : rlo + PASS],
                start=start,
                stop=stop,
            )

        ctx.enter_context(tc.manual_schedule())

        ident = const.tile([P, P], F32, name="ident")
        make_identity(nc, ident[:])

        cond_v = cond.rearrange("(g p t) k -> g p t k", p=P, t=4)
        feat_v = feat.rearrange("(g p t) n -> g p t n", p=P, t=4)
        wg_v = w_gamma.rearrange("(p j) n -> p j n", j=4)
        wb_v = w_beta.rearrange("(p j) n -> p j n", j=4)
        bytes_v = w_proj_bytes.rearrange("(g p j) r -> g p j r", p=P, j=4)
        y_v = y_out.rearrange("(g p t) r -> g t p r", p=P, t=4)

        cond_raw, feat_raw, wg_raw, wb_raw, wbytes, rows = {}, {}, {}, {}, {}, {}

        def raw4(name):
            return work.tile([P, 4, PASS], BF16, name=name, tag="raw4", bufs=4)

        def raw8(name):
            return work.tile([P, 4, 2 * PASS], BF16, name=name, tag="raw8", bufs=4)

        def load_cond(g):
            cond_raw[g] = raw4("cond_raw%d" % g)
            nc.sync.dma_start(out=cond_raw[g][:], in_=cond_v[g])

        def load_first(view, store, key, name):
            t = raw4(name)
            nc.sync.dma_start(out=t[:], in_=view[:, :, 0:PASS])
            store[key] = (t, 0)

        def load_rest(view, store, keys, name):
            t = raw8(name)
            nc.sync.dma_start(out=t[:], in_=view[:, :, PASS:N])
            store[keys[0]], store[keys[1]] = (t, 0), (t, PASS)

        def load_row(name, vec, width):
            rows[name] = const.tile([P, width], BF16, name=name)
            nc.sync.dma_start(out=rows[name][:], in_=vec.partition_broadcast(P))

        load_cond(0)
        load_first(wg_v, wg_raw, 0, "wg_raw0")
        load_first(feat_v[0], feat_raw, (0, 0), "feat_raw00")
        load_first(wb_v, wb_raw, 0, "wb_raw0")

        bg_raw = const.tile([P, 2 * CG, 2], BF16, name="bg_raw")
        bb_raw = const.tile([P, 2 * CG, 2], BF16, name="bb_raw")
        gain_raw = const.tile([P, FG, 4], BF16, name="gain_raw")
        rest_raw = const.tile([P, FG, 4], BF16, name="rest_raw")
        wsc = const.tile([P, CG, 4], F32, name="wsc")
        nc.scalar.dma_start(out=bg_raw[:], in_=b_gamma.rearrange("(a q e) -> q a e", q=P, e=2))
        nc.scalar.dma_start(out=bb_raw[:], in_=b_beta.rearrange("(a q e) -> q a e", q=P, e=2))
        nc.scalar.dma_start(out=gain_raw[:], in_=frame_gain.rearrange("(g p t) -> p g t", p=P, t=4))
        nc.scalar.dma_start(out=rest_raw[:], in_=frame_restore.rearrange("(g p t) -> p g t", p=P, t=4))
        nc.scalar.dma_start(
            out=wsc[:], in_=w_proj_scale.rearrange("(g p j) o -> p g (j o)", p=P, j=4)
        )

        load_rest(wg_v, wg_raw, (1, 2), "wg_raw12")
        load_rest(wb_v, wb_raw, (1, 2), "wb_raw12")
        load_rest(feat_v[0], feat_raw, ((0, 1), (0, 2)), "feat_raw012")

        bg1 = const.tile([P, 4 * CG], F32, name="bg1")
        bb1 = const.tile([P, 4 * CG], F32, name="bb1")
        nc.gpsimd.tensor_scalar(bg1[:], bg_raw[:].rearrange("p a e -> p (a e)"), 1.0, 0.0, op0=ALU.add, op1=ALU.add)
        nc.gpsimd.tensor_scalar(bb1[:], bb_raw[:].rearrange("p a e -> p (a e)"), 1.0, 0.0, op0=ALU.mult, op1=ALU.add)
        gain = const.tile([P, 4 * FG], F32, name="gain")
        rest = const.tile([P, 4 * FG], F32, name="rest")
        nc.gpsimd.tensor_scalar(gain[:], gain_raw[:].rearrange("p g t -> p (g t)"), SLOPE, 0.0, op0=ALU.mult, op1=ALU.add)
        nc.gpsimd.tensor_scalar(rest[:], rest_raw[:].rearrange("p g t -> p (g t)"), 1.0, 0.0, op0=ALU.mult, op1=ALU.add)

        cond_q, wg_q, wb_q, wproj_q, pool_q, hf_q, hc_q = {}, {}, {}, {}, {}, {}, {}
        groups = {}

        def cond_turn(g):
            words = cond_raw[g][:].bitcast(F32)
            grp = groups["cond", g] = group()
            gw = grp[:].bitcast(F32).rearrange("p (t f u) -> p t f u", t=4, u=2)
            for h in range(2):
                b = bank("turn")
                for t2 in range(2):
                    for u in range(2):
                        lo = (2 * t2 + u) * P
                        nc.tensor.transpose(b[:, lo : lo + P], words[:, 2 * h + t2, u::2], ident[:])
                nc.scalar.copy(
                    out=gw[:, 2 * h : 2 * h + 2],
                    in_=b[:].rearrange("p (t u f) -> p t f u", t=2, u=2),
                )

        def cond_quant(g):
            cond_q[g] = codes("cond%d" % g)
            quantize(cond_q[g], groups["cond", g][:])

        def mix(eng, dst, src):
            if eng == "v":
                nc.vector.tensor_copy(out=dst, in_=src)
            elif eng == "s":
                nc.scalar.copy(out=dst, in_=src)
            else:
                for lo in range(0, dst.shape[1], P):
                    part = slice(lo, lo + P)
                    nc.gpsimd.tensor_scalar(dst[:, part], src[:, part], 1.0, 0.0, op0=ALU.mult, op1=ALU.add)

        def w_mix(which, raw, c, eng, e):
            t, lo = raw[c]
            if e == 0:
                groups[which, c] = group()
            grp = groups[which, c]
            src = t[:, :, lo : lo + PASS].rearrange("p j (m e) -> p e m j", e=2)[:, e]
            dst = grp[:].rearrange("p (e m j) -> p e m j", e=2, j=4)[:, e]
            mix(eng, dst, src)

        def w_quant(which, store, c):
            store[c] = codes("%s%d" % (which, c))
            quantize(store[c], groups[which, c][:])

        def wp_widen(c, h):
            wide = groups["wide", c, h] = work.tile([P, 4, PASS], BF16, name="wide", tag="wide", bufs=3)
            for j in range(4):
                nc.scalar.activation(
                    out=wide[:, j, :],
                    in_=wbytes[c][:, j, h * PASS : (h + 1) * PASS].bitcast(FP8),
                    func=ACT.Copy,
                    scale=wsc[:, c, j : j + 1],
                )

        def wp_mix(c, h, eng="v"):
            grp = groups["wp", c, h] = group()
            dst = grp[:].rearrange("p (r j) -> p r j", j=4)
            src = groups["wide", c, h][:].rearrange("p j r -> p r j")
            mix(eng, dst, src)

        def wp_quant(c, h):
            if h == 0:
                wproj_q[c] = codes("wproj%d" % c, R)
            quantize(wproj_q[c], groups["wp", c, h][:], h * PASS)

        pool_raw = {}

        def pool_turn(g):
            words = pool_raw[0][:].bitcast(F32)
            grp = groups["pool", g] = group()
            gw = grp[:].bitcast(F32).rearrange("p (i s u) -> p i s u", i=4, u=2)
            for h in range(2):
                b = bank("turn")
                for i2 in range(2):
                    for u in range(2):
                        lo = (2 * i2 + u) * P
                        nc.tensor.transpose(
                            b[:, lo : lo + P],
                            words[:, 2 * h + i2, 256 * g + u : 256 * (g + 1) : 2],
                            ident[:],
                        )
                nc.scalar.copy(
                    out=gw[:, 2 * h : 2 * h + 2],
                    in_=b[:].rearrange("p (i u s) -> p i s u", i=2, u=2),
                )

        def pool_quant(g):
            pool_q[g] = codes("pool%d" % g)
            quantize(pool_q[g], groups["pool", g][:])

        blocks = [(g, c) for g in range(FG) for c in range(CG)]
        ft, pair, a_t, f_t, r_t, fb_t, hf_t, hc_t = {}, {}, {}, {}, {}, {}, {}, {}

        def feat_turn(b):
            t, lo = feat_raw[blocks[b]]
            words = t[:].bitcast(F32)
            ft[b] = work.tile([P, 2, PASS], F32, name="feat_t", tag="feat_t", bufs=2)
            for v in range(2):
                ps = bank("turn")
                for tt in range(4):
                    w0 = lo // 2 + v * P
                    nc.tensor.transpose(ps[:, tt * P : (tt + 1) * P], words[:, tt, w0 : w0 + P], ident[:])
                nc.scalar.copy(out=ft[b][:, v, :], in_=ps[:])

        def film_mx(b, i):
            g, c = blocks[b]
            e, v = i // 2, i % 2
            pg, pb = bank("mx"), bank("mx")
            mx(pg[:], wg_q[c], i * P, cond_q[g], 0, True, True)
            mx(pb[:], wb_q[c], i * P, cond_q[g], 0, True, True)
            pair[b, i] = (pg, pb)

        def film_scale(b, i):
            g, c = blocks[b]
            e, v = i // 2, i % 2
            idx = 4 * c + 2 * v + e
            fb = ft[b][:, v, :].bitcast(BF16).rearrange("p (f e) -> p e f", e=2)
            a_t[b, i] = work.tile([P, PASS], F32, name="a", tag="a", bufs=3)
            nc.vector.scalar_tensor_tensor(
                out=a_t[b, i][:], in0=pair[b, i][0][:], scalar=bg1[:, idx : idx + 1], in1=fb[:, e, :],
                op0=ALU.add, op1=ALU.mult,
            )

        def film_shift(b, i):
            g, c = blocks[b]
            e, v = i // 2, i % 2
            idx = 4 * c + 2 * v + e
            f_t[b, i] = work.tile([P, PASS], F32, name="f", tag="f", bufs=5)
            nc.vector.scalar_tensor_tensor(
                out=f_t[b, i][:], in0=pair[b, i][1][:], scalar=bb1[:, idx : idx + 1], in1=a_t[b, i][:],
                op0=ALU.add, op1=ALU.add,
            )

        def relu(b, i):
            r_t[b, i] = work.tile([P, PASS], F32, name="r", tag="r", bufs=4)
            eng = ENG.get("relu%d%d" % (b, i), "s")
            if eng == "g":
                nc.gpsimd.tensor_scalar(r_t[b, i][:], f_t[b, i][:], 0.0, 1.0 / SLOPE - 1.0, op0=ALU.max, op1=ALU.mult)
            elif eng == "s":
                nc.scalar.activation(out=r_t[b, i][:], in_=f_t[b, i][:], func=ACT.Relu, scale=1.0 / SLOPE - 1.0)
            else:
                nc.vector.tensor_scalar(r_t[b, i][:], f_t[b, i][:], 0.0, 1.0 / SLOPE - 1.0, op0=ALU.max, op1=ALU.mult)

        def f_turn(b, i):
            ps = fb_t[b, i] = bank("fin")
            for t in range(4):
                part = slice(t * P, (t + 1) * P)
                nc.tensor.matmul(ps[:, part], f_t[b, i][:, part], ident[:], start=True, stop=False, is_transpose=True)
                nc.tensor.matmul(ps[:, part], r_t[b, i][:, part], ident[:], start=False, stop=True, is_transpose=True)

        def finish(b, i):
            g, c = blocks[b]
            e, v = i // 2, i % 2
            if i == 0:
                hf_t[b] = work.tile([P, 4 * PASS], BF16, name="hf", tag="hf", bufs=2, align_bytes=64)
            nc.vector.tensor_tensor(
                hf_t[b][:].rearrange("p (jh e v qh t) -> p jh e v qh t", jh=2, e=2, v=2, t=4)[:, :, e, v],
                fb_t[b, i][:].rearrange("p (t qh jh) -> p jh qh t", t=4, jh=2),
                gain[:, 4 * g : 4 * g + 4].unsqueeze(1).unsqueeze(1).to_broadcast([P, 2, 64, 4]),
                op=ALU.mult,
            )

        def hf_quant(b):
            hf_q[blocks[b]] = codes("hf%d%d" % blocks[b])
            quantize(hf_q[blocks[b]], hf_t[b][:])

        def hc_turn(b, u):
            if u == 0:
                hc_t[b] = work.tile([P, 4 * PASS], BF16, name="hc", tag="hc", bufs=2, align_bytes=64)
            words = hf_t[b][:].bitcast(F32)
            ps = bank("turn")
            for j in range(4):
                nc.tensor.transpose(
                    ps[:, j * P : (j + 1) * P], words[:, 256 * j + u : 256 * (j + 1) : 2], ident[:]
                )
            nc.scalar.copy(
                out=hc_t[b][:, 1024 * u : 1024 * (u + 1)].rearrange("q (e p j) -> q e p j", e=2, j=4),
                in_=ps[:].bitcast(BF16).rearrange("q (j p e) -> q e p j", j=4, e=2),
            )

        def hc_quant(b, u):
            if u == 0:
                hc_q[blocks[b]] = codes("hc%d%d" % blocks[b])
            q = hc_q[blocks[b]]
            nc.vector.quantize_mx(
                out=q[0][:, 256 * u : 256 * (u + 1)].bitcast(FP8X4),
                scales=q[1][:, 256 * u : 256 * (u + 1)],
                in_=hc_t[b][:, 1024 * u : 1024 * (u + 1)],
            )

        ys_t, yb, zb = {}, {}, {}

        def y_mx(g, t, h, c0=0, c1=CG, tag="mx"):
            if c0 == 0:
                yb[g, t, h] = bank(tag)
            for c in range(c0, c1):
                mx(yb[g, t, h][:], hc_q[g, c], t * P, wproj_q[c], h * PASS, c == 0, c == CG - 1)

        def y_out_half(g, t, h):
            if h == 0:
                ys_t[g, t] = work.tile([P, R], F32, name="ys", tag="raw4", bufs=4)
            ys = ys_t[g, t]
            half = slice(h * PASS, (h + 1) * PASS)
            scale = rest[:, 4 * g + t : 4 * g + t + 1]
            if ENG.get("y%d%d%d" % (g, t, h), "v") == "v":
                nc.vector.scalar_tensor_tensor(
                    out=ys[:, half], in0=yb[g, t, h][:], scalar=scale,
                    in1=rows["bias_row"][:, half], op0=ALU.mult, op1=ALU.add,
                )
            else:
                nc.scalar.activation(out=ys[:, half], in_=yb[g, t, h][:], func=ACT.Copy, scale=scale)
                nc.gpsimd.tensor_tensor(ys[:, half], ys[:, half], rows["bias_row"][:, half], op=ALU.add)
            if h == 1:
                nc.sync.dma_start(out=y_v[g, t], in_=ys[:])

        def z_mx(c, i, tag="mx"):
            zb[c, i] = bank(tag)
            for g in range(FG):
                mx(zb[c, i][:], pool_q[g], i * P, hf_q[g, c], 0, g == 0, g == FG - 1)

        def z_store(c, i):
            zs = work.tile([P, PASS], F32, name="zs", tag="zs", bufs=6)
            row = rows["cgain_row"][:, c * PASS : (c + 1) * PASS]
            zn = zs[:].rearrange("s (q j) -> s q j", j=4)
            zp = zb[c, i][:].rearrange("s (j q) -> s q j", j=4)
            if ENG.get("z%d%d" % (c, i), "v") == "v":
                nc.vector.tensor_tensor(zn, zp, row.rearrange("s (q j) -> s q j", j=4), op=ALU.mult)
            else:
                nc.scalar.copy(out=zn, in_=zp)
                nc.gpsimd.tensor_tensor(zs[:], zs[:], row, op=ALU.mult)
            nc.sync.dma_start(out=z_out[i * P : (i + 1) * P, c * PASS : (c + 1) * PASS], in_=zs[:])

        jobs, issued = [], []

        def issue(n):
            for _ in range(n):
                if jobs:
                    job = jobs.pop(0)
                    job[0]()
                    issued.append(job)

        def drain(n=1):
            for _ in range(n):
                if issued:
                    issued.pop(0)[1]()

        def slot(fns=()):
            for fn in fns:
                fn()

        def load_w_proj(c):
            wbytes[c] = const.tile([P, 4, R], U8, name="w_bytes%d" % c)
            nc.sync.dma_start(out=wbytes[c][:], in_=bytes_v[c])

        def load_pool():
            pool_raw[0] = raw8("pool_raw")
            nc.sync.dma_start(out=pool_raw[0][:], in_=w_pool.rearrange("(i s) m -> s i m", s=P))

        extras = {"go": lambda: issue(1), "out": lambda: drain(1)}
        for c in range(CG):
            for which, raw, store in (("wg", wg_raw, wg_q), ("wb", wb_raw, wb_q)):
                for e in range(2):
                    n = "%s%d%d" % (which, c, e)
                    extras[n] = lambda which=which, raw=raw, c=c, e=e, n=n: w_mix(which, raw, c, ENG.get(n, "s"), e)
                extras["q%s%d" % (which, c)] = lambda which=which, store=store, c=c: w_quant(which, store, c)
            for h in range(2):
                k = 2 * c + h
                extras["wd%d" % k] = lambda c=c, h=h: wp_widen(c, h)
                extras["wm%d" % k] = lambda c=c, h=h, k=k: wp_mix(c, h, ENG.get("wm%d" % k, "v"))
                extras["wq%d" % k] = lambda c=c, h=h: wp_quant(c, h)
        for g in range(FG):
            extras["ct%d" % g] = lambda g=g: cond_turn(g)
            extras["cq%d" % g] = lambda g=g: cond_quant(g)
            extras["pt%d" % g] = lambda g=g: pool_turn(g)
            extras["pq%d" % g] = lambda g=g: pool_quant(g)

        def do(names):
            for n in names.split():
                extras[n]()

        def add_y(g, lo, hi):
            for t, h in [(t, h) for t in range(4) for h in range(2)][lo:hi]:
                jobs.append((lambda t=t, h=h: y_mx(g, t, h), lambda t=t, h=h: y_out_half(g, t, h)))

        def add_z(c):
            for i in range(4):
                jobs.append((lambda i=i: z_mx(c, i), lambda i=i: z_store(c, i)))

        add_y(0, 0, 8)
        add_z(0)
        add_z(1)
        add_z(2)

        tiles = [(b, i) for b in range(len(blocks)) for i in range(4)]
        NT = len(tiles)

        def loads(n):
            if n == 2:
                load_cond(1)
                load_first(feat_v[1], feat_raw, (1, 0), "feat_raw10")
                load_pool()
            if n == 6:
                load_rest(feat_v[1], feat_raw, ((1, 1), (1, 2)), "feat_raw112")
                load_row("bias_row", b_proj, R)
                load_row("cgain_row", chan_gain, N)

        def stage(n, x):
            if n < NT:
                film_scale(*tiles[n])
            do(x[0])
            if 0 <= n - 1 < NT:
                film_shift(*tiles[n - 1])
            if 0 <= n + 1 < NT:
                film_mx(*tiles[n + 1])
            if 0 <= n - 1 < NT:
                relu(*tiles[n - 1])
            if n % 4 == 1 and n // 4 + 1 < len(blocks):
                feat_turn(n // 4 + 1)
            if 0 <= n - 2 < NT:
                f_turn(*tiles[n - 2])
            do(x[1])
            if 0 <= n - 3 < NT:
                finish(*tiles[n - 3])
            do(x[2])
            loads(n)

        for k in range(8):
            for tag in ("mx", "turn", "fin"):
                extras["p%d%s" % (k, tag)] = lambda k=k, tag=tag: y_mx(1, k // 2, k % 2, 0, 2, tag)
            extras["f%d" % k] = lambda k=k: y_mx(1, k // 2, k % 2, 2, 3)
            extras["o%d" % k] = lambda k=k: y_out_half(1, k // 2, k % 2)
        for b in range(len(blocks)):
            extras["hf%d" % b] = lambda b=b: hf_quant(b)
            for u in range(2):
                extras["ht%d%d" % (b, u)] = lambda b=b, u=u: hc_turn(b, u)
                extras["hq%d%d" % (b, u)] = lambda b=b, u=u: hc_quant(b, u)

        cond_turn(0)
        do("wg00 wg01")
        cond_quant(0)
        do("wb00 wb01")
        feat_turn(0)
        do("qwg0 qwb0")
        film_mx(*tiles[0])
        for c in range(CG):
            load_w_proj(c)
        for n in range(NT + 3):
            stage(n, PLAN[n])
        do(TAIL)
